import numpy as np, ml_dtypes
CORES = [13,21,141,149]
N = 4
import mx_ref
NC, WT = 256, 2
LR = np.float32(2.0 ** -2)
BF = ml_dtypes.bfloat16
def cut(t, i, w=512):
    return t[:, w * i:w * i + w]
def setup_inputs(rng):
    def f(*shape):
        return mx_ref.flush((rng.standard_normal(shape, dtype=np.float32) * np.exp2(rng.integers(-2, 3, shape[:-1] + (1,)))).astype(BF))
    return {"w": f(N, 128, WT * 512), "gr": f(N, 128, WT * 512), "x": f(N, 128, 4 * NC)}
def setup_inputs_blocks(rng):
    d = setup_inputs(rng)
    for k in ("x",): d[k] = mx_ref.spread(d[k], rng, 4)
    for k in ("w", "gr"): d[k] = mx_ref.spread(d[k], rng, 2)
    return d
def setup_inputs_wide(rng):
    d = setup_inputs(rng)
    for k in ("w", "gr", "x"): d[k] = mx_ref.flush((d[k].astype(np.float32) * np.exp2(rng.integers(-4, 5, (N, 1, 1))).astype(np.float32)).astype(BF))
    return d
def setup_inputs_faint(rng):
    d = setup_inputs(rng); d["gr"] = mx_ref.flush((d["gr"].astype(np.float32) * np.float32(2.0 ** -12)).astype(BF))
    return d
def reference(w, gr, x):
    H = [mx_ref.quantize((cut(w[j], i).astype(np.float32) - cut(gr[j], i).astype(np.float32) * LR).astype(BF)) for j in range(N) for i in range(WT)]
    y = np.zeros((N, 128, N * WT * NC), np.float32)
    for r in range(N):
        X = mx_ref.quantize(x[r])
        for b in range(N * WT):
            y[r][:, NC * b:NC * b + NC] = mx_ref.matmul(H[b], X)
    return {"y": y}

@@ -1,0 +1,157 @@
+from concourse.bass import DstId, RemoteDMATransfer
+from concourse.mybir import dt, AluOpType, ActivationFunctionType
+
+N, WT, NC, TW = 4, 2, 256, 512
+SIM_CORES = 256
+QW = TW // 4
+
+SCRATCH = {
+    "wt": ("sbuf", [128, WT * TW], "bfloat16"),
+    "gt": ("sbuf", [128, WT * TW], "bfloat16"),
+    "gs": ("sbuf", [128, WT * TW], "bfloat16"),
+    "vt": ("sbuf", [128, WT * TW], "bfloat16"),
+    "xt": ("sbuf", [128, 4 * NC], "bfloat16"),
+    "xc": ("sbuf", [128, NC], "float8_e4m3fn_x4"),
+    "xs": ("sbuf", [128, NC], "uint8"),
+    "yt": ("sbuf", [128, N * WT * NC], "float32"),
+    "ps": ("psum", [128, 512 * N * WT], "float32"),
+}
+for _j in range(N):
+    SCRATCH["cd%d" % _j] = ("sbuf", [128, WT * QW], "float8_e4m3fn_x4")
+    SCRATCH["pl%d" % _j] = ("sbuf", [128, WT * QW], "uint8")
+
+SEMAPHORES = ["lw0", "lw1", "lg0", "lg1", "lx", "gs0", "gs1", "v0", "v1", "q0", "q1", "qx", "sent"]
+for _j in range(N):
+    SEMAPHORES += ["c0_%d" % _j, "c1_%d" % _j, "p_%d" % _j]
+    SEMAPHORES += ["m0_%d" % _j, "m1_%d" % _j, "e0_%d" % _j, "e1_%d" % _j, "st_%d" % _j]
+
+
+def _bits(mask):
+    return bin(mask).count("1")
+
+
+def _plan(src, cores, topo):
+    peers = [c for c in cores if c != src]
+    near = [c for c in peers if topo.may_write(src, c)]
+    far = [c for c in peers if not topo.may_write(src, c)]
+    relays = [c for c in range(SIM_CORES)
+              if topo.host(c) == topo.host(src) and topo.chip(c) == topo.chip(src) and c not in cores
+              and all(topo.may_write(c, d) for d in far)]
+    first = [c for c in relays if topo.die(c) != topo.die(src)][:len(far)]
+    second = [c for c in relays if topo.die(c) == topo.die(src)][:len(far)]
+    return near, far, first, second
+
+
+def rank_program(g, core, T, topo):
+    cores = [int(c) for c in T.cores]
+
+    def codes(j, a, b):
+        return T["cd%d" % j][:, a * QW:b * QW]
+
+    def plane(j, a, b):
+        return T["pl%d" % j][:, a * QW:b * QW]
+
+    def raw(j, a, b):
+        return codes(j, a, b).bitcast(dt.uint8)
+
+    def send(view, dsts, sem):
+        mask = topo.mask(core, dsts[0])
+        for d in dsts:
+            mask &= topo.mask(core, d)
+        ids = []
+        for d in dsts:
+            rid, pid = topo.addr(d, core)
+            ids.append(DstId(rid=rid, pnc=pid))
+        g.remote_dma_fused([RemoteDMATransfer(dst_ids=ids, dma_engine_mask=mask, remote_sem=sem,
+                                              srcs=[view], dsts=[view for d in dsts])], local_sem=T.sem.sent)
+        return _bits(mask)
+
+    rank = T.rank_of(core)
+    if rank is None:
+        for j, src in enumerate(cores):
+            near, far, first, second = _plan(src, cores, topo)
+            hop = _bits(topo.mask(src, core)) if core in first + second else 0
+            sent = 0
+            if core in first:
+                d = far[first.index(core)]
+                g.wait_ge(T.sem["c0_%d" % j], hop)
+                sent += send(raw(j, 0, 1), [d], T.sem["c0_%d" % j])
+                g.wait_ge(T.sem["p_%d" % j], hop)
+                sent += send(plane(j, 0, 2), [d], T.sem["p_%d" % j])
+            if core in second:
+                d = far[second.index(core)]
+                g.wait_ge(T.sem["c1_%d" % j], hop)
+                sent += send(raw(j, 1, 2), [d], T.sem["c1_%d" % j])
+            if sent:
+                g.wait_ge(T.sem.sent, sent)
+        return
+
+    near, far, first, second = _plan(core, cores, topo)
+    r = rank
+    t0, t1 = slice(0, TW), slice(TW, 2 * TW)
+
+    g.sync.dma_start(T.gt[:, t0], T.gr[:, t0]).then_inc(T.sem.lg0, 16)
+    g.scalar.dma_start(T.wt[:, t0], T.w[:, t0]).then_inc(T.sem.lw0, 16)
+    g.sync.dma_start(T.gt[:, t1], T.gr[:, t1]).then_inc(T.sem.lg1, 16)
+    g.scalar.dma_start(T.wt[:, t1], T.w[:, t1]).then_inc(T.sem.lw1, 16)
+    g.sync.dma_start(T.xt[:], T.x[:]).then_inc(T.sem.lx, 16)
+
+    g.scalar.wait_ge(T.sem.lg1, 16)
+    g.scalar.activation(T.gs[:, t1], T.gt[:, t1], ActivationFunctionType.Copy, scale=0.25).then_inc(T.sem.gs1, 1)
+    g.vector.wait_ge(T.sem.lg0, 16)
+    g.vector.tensor_scalar(T.gs[:, t0], T.gt[:, t0], 0.25, None, AluOpType.mult).then_inc(T.sem.gs0, 1)
+    for i, t in ((0, t0), (1, t1)):
+        g.vector.wait_ge(T.sem["lw%d" % i], 16)
+        g.vector.wait_ge(T.sem["gs%d" % i], 1)
+        g.vector.tensor_tensor(T.vt[:, t], T.wt[:, t], T.gs[:, t], AluOpType.subtract).then_inc(T.sem["v%d" % i], 1)
+        g.vector.wait_ge(T.sem["v%d" % i], 1)
+        g.vector.quantize_mx(codes(r, i, i + 1), plane(r, i, i + 1), T.vt[:, t]).then_inc(T.sem["q%d" % i], 1)
+    g.vector.wait_ge(T.sem.lx, 16)
+    g.vector.quantize_mx(T.xc[:], T.xs[:], T.xt[:]).then_inc(T.sem.qx, 1)
+
+    g.wait_ge(T.sem.q0, 1)
+    sent = send(raw(r, 0, 1), first, T.sem["c0_%d" % r])
+    g.wait_ge(T.sem.q1, 1)
+    sent += send(raw(r, 1, 2), second, T.sem["c1_%d" % r])
+    sent += send(plane(r, 0, 2), first, T.sem["p_%d" % r])
+    sent += send(raw(r, 0, 2), near, T.sem["c0_%d" % r])
+    sent += send(plane(r, 0, 2), near, T.sem["p_%d" % r])
+    g.wait_ge(T.sem.sent, sent)
+
+    order = [r] + [cores.index(c) for c in near] + [cores.index(c) for c in far]
+    g.tensor.wait_ge(T.sem.qx, 1)
+    for j in order:
+        src = cores[j]
+        if src in far:
+            _, jfar, jfirst, jsecond = _plan(src, cores, topo)
+            k = jfar.index(core)
+            e0, e1 = _bits(topo.mask(jfirst[k], core)), _bits(topo.mask(jsecond[k], core))
+        elif src in near:
+            e0 = _bits(topo.mask(src, core))
+        for i in range(WT):
+            if j == r:
+                g.tensor.wait_ge(T.sem["q%d" % i], 1)
+            elif i == 0:
+                g.tensor.wait_ge(T.sem["c0_%d" % j], e0)
+                g.tensor.wait_ge(T.sem["p_%d" % j], e0)
+            elif src in far:
+                g.tensor.wait_ge(T.sem["c1_%d" % j], e1)
+            b = WT * j + i
+            g.tensor.matmul_mx(T.ps[:, 512 * b:512 * b + NC], codes(j, i, i + 1), plane(j, i, i + 1), T.xc[:], T.xs[:],
+                               True, True).then_inc(T.sem["m%d_%d" % (i, j)], 1)
+
+    for j in order:
+        b = WT * j
+        ya, yb = slice(NC * b, NC * b + NC), slice(NC * b + NC, NC * b + 2 * NC)
+        g.vector.wait_ge(T.sem["m0_%d" % j], 1)
+        g.vector.tensor_copy(T.yt[:, ya], T.ps[:, 512 * b:512 * b + NC]).then_inc(T.sem["e0_%d" % j], 1)
+        g.scalar.wait_ge(T.sem["m1_%d" % j], 1)
+        g.scalar.activation(T.yt[:, yb], T.ps[:, 512 * b + 512:512 * b + 512 + NC],
+                            ActivationFunctionType.Copy).then_inc(T.sem["e1_%d" % j], 1)
+        q = g.scalar if j == order[-1] else g.sync
+        q.wait_ge(T.sem["e0_%d" % j], 1)
+        q.wait_ge(T.sem["e1_%d" % j], 1)
+        q.dma_start(T.y[:, NC * b:NC * b + 2 * NC], T.yt[:, NC * b:NC * b + 2 * NC]).then_inc(T.sem["st_%d" % j], 16)
+    for j in order:
+        q = g.scalar if j == order[-1] else g.sync
+        q.wait_ge(T.sem["st_%d" % j], 16)

@@ -4,6 +4,11 @@ from concourse.mybir import dt, AluOpType, ActivationFunctionType
 N, WT, NC, TW = 4, 2, 256, 512
 SIM_CORES = 256
 QW = TW // 4
+HC = NC // 2
+BANK = 512
+CUT = 352
+ITEMS = ("c0", "p0", "c1", "p1")
+VIA = {"c": ((0, (0,)), (1, (1,))), "p": ((2, (0, 1)),)}
 
 SCRATCH = {
     "wt": ("sbuf", [128, WT * TW], "bfloat16"),
@@ -14,16 +19,17 @@ SCRATCH = {
     "xc": ("sbuf", [128, NC], "float8_e4m3fn_x4"),
     "xs": ("sbuf", [128, NC], "uint8"),
     "yt": ("sbuf", [128, N * WT * NC], "float32"),
-    "ps": ("psum", [128, 512 * N * WT], "float32"),
+    "ps": ("psum", [128, BANK * N * WT], "float32"),
 }
 for _j in range(N):
     SCRATCH["cd%d" % _j] = ("sbuf", [128, WT * QW], "float8_e4m3fn_x4")
     SCRATCH["pl%d" % _j] = ("sbuf", [128, WT * QW], "uint8")
 
-SEMAPHORES = ["lw0", "lw1", "lg0", "lg1", "lx", "gs0", "gs1", "v0", "v1", "q0", "q1", "qx", "sent"]
+SEMAPHORES = ["lw0", "lw1", "lg0", "lg1", "lx", "gs0", "gs0b", "gs1", "v0", "v1", "q0", "q1", "qx", "sent"]
 for _j in range(N):
-    SEMAPHORES += ["c0_%d" % _j, "c1_%d" % _j, "p_%d" % _j]
-    SEMAPHORES += ["m0_%d" % _j, "m1_%d" % _j, "e0_%d" % _j, "e1_%d" % _j, "st_%d" % _j]
+    SEMAPHORES += ["%s_%d" % (_it, _j) for _it in ITEMS]
+for _b in range(N * WT):
+    SEMAPHORES += ["m_%d" % _b, "n_%d" % _b, "e_%d" % _b, "f_%d" % _b, "s_%d" % _b]
 
 
 def _bits(mask):
@@ -33,60 +39,64 @@ def _bits(mask):
 def _plan(src, cores, topo):
     peers = [c for c in cores if c != src]
     near = [c for c in peers if topo.may_write(src, c)]
-    far = [c for c in peers if not topo.may_write(src, c)]
-    relays = [c for c in range(SIM_CORES)
-              if topo.host(c) == topo.host(src) and topo.chip(c) == topo.chip(src) and c not in cores
-              and all(topo.may_write(c, d) for d in far)]
-    first = [c for c in relays if topo.die(c) != topo.die(src)][:len(far)]
-    second = [c for c in relays if topo.die(c) == topo.die(src)][:len(far)]
-    return near, far, first, second
+    far = sorted((c for c in peers if not topo.may_write(src, c)), key=lambda c: topo.host(c) != topo.host(src))
+    fit = [c for c in range(SIM_CORES)
+           if topo.host(c) == topo.host(src) and topo.chip(c) == topo.chip(src) and c not in cores
+           and all(topo.may_write(c, d) for d in far)]
+    own = [c for c in fit if topo.die(c) == topo.die(src)]
+    other = [c for c in fit if topo.die(c) != topo.die(src)]
+    return near, far, [other[0], own[0], other[1]]
+
+
+def _common(src, dsts, topo):
+    mask = topo.mask(src, dsts[0])
+    for d in dsts:
+        mask &= topo.mask(src, d)
+    return mask
+
+
+def _relay_mask(src, item, cores, topo):
+    near, _, relays = _plan(src, cores, topo)
+    mask = _common(src, relays, topo)
+    return mask & ~_common(src, near, topo) if item[1] == "0" else mask
 
 
 def rank_program(g, core, T, topo):
     cores = [int(c) for c in T.cores]
 
-    def codes(j, a, b):
-        return T["cd%d" % j][:, a * QW:b * QW]
+    def codes(j, i):
+        return T["cd%d" % j][:, i * QW:(i + 1) * QW]
 
-    def plane(j, a, b):
-        return T["pl%d" % j][:, a * QW:b * QW]
+    def plane(j, i):
+        return T["pl%d" % j][:, i * QW:(i + 1) * QW]
 
-    def raw(j, a, b):
-        return codes(j, a, b).bitcast(dt.uint8)
-
-    def send(view, dsts, sem):
-        mask = topo.mask(core, dsts[0])
-        for d in dsts:
-            mask &= topo.mask(core, d)
+    def send(j, item, dsts, mask):
+        i = int(item[1])
+        view = codes(j, i).bitcast(dt.uint8) if item[0] == "c" else plane(j, i)
         ids = []
         for d in dsts:
             rid, pid = topo.addr(d, core)
             ids.append(DstId(rid=rid, pnc=pid))
-        g.remote_dma_fused([RemoteDMATransfer(dst_ids=ids, dma_engine_mask=mask, remote_sem=sem,
+        g.remote_dma_fused([RemoteDMATransfer(dst_ids=ids, dma_engine_mask=mask, remote_sem=T.sem["%s_%d" % (item, j)],
                                               srcs=[view], dsts=[view for d in dsts])], local_sem=T.sem.sent)
         return _bits(mask)
 
     rank = T.rank_of(core)
     if rank is None:
         for j, src in enumerate(cores):
-            near, far, first, second = _plan(src, cores, topo)
-            hop = _bits(topo.mask(src, core)) if core in first + second else 0
+            _, far, relays = _plan(src, cores, topo)
             sent = 0
-            if core in first:
-                d = far[first.index(core)]
-                g.wait_ge(T.sem["c0_%d" % j], hop)
-                sent += send(raw(j, 0, 1), [d], T.sem["c0_%d" % j])
-                g.wait_ge(T.sem["p_%d" % j], hop)
-                sent += send(plane(j, 0, 2), [d], T.sem["p_%d" % j])
-            if core in second:
-                d = far[second.index(core)]
-                g.wait_ge(T.sem["c1_%d" % j], hop)
-                sent += send(raw(j, 1, 2), [d], T.sem["c1_%d" % j])
+            for item in ITEMS:
+                for k, serves in VIA[item[0]]:
+                    if relays[k] == core:
+                        dsts = [far[f] for f in serves]
+                        g.wait_ge(T.sem["%s_%d" % (item, j)], _bits(_relay_mask(src, item, cores, topo)))
+                        sent += send(j, item, dsts, _common(core, dsts, topo))
             if sent:
                 g.wait_ge(T.sem.sent, sent)
         return
 
-    near, far, first, second = _plan(core, cores, topo)
+    near, far, relays = _plan(core, cores, topo)
     r = rank
     t0, t1 = slice(0, TW), slice(TW, 2 * TW)
 
@@ -96,62 +106,95 @@ def rank_program(g, core, T, topo):
     g.scalar.dma_start(T.wt[:, t1], T.w[:, t1]).then_inc(T.sem.lw1, 16)
     g.sync.dma_start(T.xt[:], T.x[:]).then_inc(T.sem.lx, 16)
 
+    a, b = slice(0, CUT), slice(CUT, TW)
+    g.scalar.wait_ge(T.sem.lg0, 16)
+    g.scalar.activation(T.gs[:, b], T.gt[:, b], ActivationFunctionType.Copy, scale=0.25).then_inc(T.sem.gs0b, 1)
     g.scalar.wait_ge(T.sem.lg1, 16)
     g.scalar.activation(T.gs[:, t1], T.gt[:, t1], ActivationFunctionType.Copy, scale=0.25).then_inc(T.sem.gs1, 1)
     g.vector.wait_ge(T.sem.lg0, 16)
-    g.vector.tensor_scalar(T.gs[:, t0], T.gt[:, t0], 0.25, None, AluOpType.mult).then_inc(T.sem.gs0, 1)
+    g.vector.tensor_scalar(T.gs[:, a], T.gt[:, a], 0.25, None, AluOpType.mult).then_inc(T.sem.gs0, 1)
     for i, t in ((0, t0), (1, t1)):
         g.vector.wait_ge(T.sem["lw%d" % i], 16)
         g.vector.wait_ge(T.sem["gs%d" % i], 1)
+        if i == 0:
+            g.vector.wait_ge(T.sem.gs0b, 1)
         g.vector.tensor_tensor(T.vt[:, t], T.wt[:, t], T.gs[:, t], AluOpType.subtract).then_inc(T.sem["v%d" % i], 1)
         g.vector.wait_ge(T.sem["v%d" % i], 1)
-        g.vector.quantize_mx(codes(r, i, i + 1), plane(r, i, i + 1), T.vt[:, t]).then_inc(T.sem["q%d" % i], 1)
+        g.vector.quantize_mx(codes(r, i), plane(r, i), T.vt[:, t]).then_inc(T.sem["q%d" % i], 1)
     g.vector.wait_ge(T.sem.lx, 16)
     g.vector.quantize_mx(T.xc[:], T.xs[:], T.xt[:]).then_inc(T.sem.qx, 1)
 
-    g.wait_ge(T.sem.q0, 1)
-    sent = send(raw(r, 0, 1), first, T.sem["c0_%d" % r])
-    g.wait_ge(T.sem.q1, 1)
-    sent += send(raw(r, 1, 2), second, T.sem["c1_%d" % r])
-    sent += send(plane(r, 0, 2), first, T.sem["p_%d" % r])
-    sent += send(raw(r, 0, 2), near, T.sem["c0_%d" % r])
-    sent += send(plane(r, 0, 2), near, T.sem["p_%d" % r])
+    near_mask = _common(core, near, topo)
+    sent = 0
+    for i in range(WT):
+        g.wait_ge(T.sem["q%d" % i], 1)
+        items = ["c%d" % i, "p%d" % i]
+        for item in items:
+            sent += send(r, item, [relays[k] for k, _ in VIA[item[0]]], _relay_mask(core, item, cores, topo))
+        for item in items:
+            sent += send(r, item, near, near_mask)
     g.wait_ge(T.sem.sent, sent)
 
-    order = [r] + [cores.index(c) for c in near] + [cores.index(c) for c in far]
-    g.tensor.wait_ge(T.sem.qx, 1)
-    for j in order:
-        src = cores[j]
-        if src in far:
-            _, jfar, jfirst, jsecond = _plan(src, cores, topo)
-            k = jfar.index(core)
-            e0, e1 = _bits(topo.mask(jfirst[k], core)), _bits(topo.mask(jsecond[k], core))
-        elif src in near:
-            e0 = _bits(topo.mask(src, core))
-        for i in range(WT):
-            if j == r:
-                g.tensor.wait_ge(T.sem["q%d" % i], 1)
-            elif i == 0:
-                g.tensor.wait_ge(T.sem["c0_%d" % j], e0)
-                g.tensor.wait_ge(T.sem["p_%d" % j], e0)
-            elif src in far:
-                g.tensor.wait_ge(T.sem["c1_%d" % j], e1)
-            b = WT * j + i
-            g.tensor.matmul_mx(T.ps[:, 512 * b:512 * b + NC], codes(j, i, i + 1), plane(j, i, i + 1), T.xc[:], T.xs[:],
-                               True, True).then_inc(T.sem["m%d_%d" % (i, j)], 1)
+    nearj, farj = [cores.index(c) for c in near], [cores.index(c) for c in far]
+    whole = [(j, i) for j in [r] + nearj for i in range(WT)] + [(j, 0) for j in farj]
+    halved = [(j, 1) for j in farj]
+    spare = [WT * r + k for k in range(len(halved))]
 
-    for j in order:
-        b = WT * j
-        ya, yb = slice(NC * b, NC * b + NC), slice(NC * b + NC, NC * b + 2 * NC)
-        g.vector.wait_ge(T.sem["m0_%d" % j], 1)
-        g.vector.tensor_copy(T.yt[:, ya], T.ps[:, 512 * b:512 * b + NC]).then_inc(T.sem["e0_%d" % j], 1)
-        g.scalar.wait_ge(T.sem["m1_%d" % j], 1)
-        g.scalar.activation(T.yt[:, yb], T.ps[:, 512 * b + 512:512 * b + 512 + NC],
-                            ActivationFunctionType.Copy).then_inc(T.sem["e1_%d" % j], 1)
-        q = g.scalar if j == order[-1] else g.sync
-        q.wait_ge(T.sem["e0_%d" % j], 1)
-        q.wait_ge(T.sem["e1_%d" % j], 1)
-        q.dma_start(T.y[:, NC * b:NC * b + 2 * NC], T.yt[:, NC * b:NC * b + 2 * NC]).then_inc(T.sem["st_%d" % j], 16)
-    for j in order:
-        q = g.scalar if j == order[-1] else g.sync
-        q.wait_ge(T.sem["st_%d" % j], 16)
+    g.tensor.wait_ge(T.sem.qx, 1)
+    for j, i in whole + halved:
+        src = cores[j]
+        if j == r:
+            g.tensor.wait_ge(T.sem["q%d" % i], 1)
+        else:
+            for item in ("c%d" % i, "p%d" % i):
+                if j in nearj:
+                    n = _bits(_common(src, [core], topo))
+                else:
+                    _, jfar, jrelays = _plan(src, cores, topo)
+                    f = jfar.index(core)
+                    n = [_bits(_common(jrelays[k], [jfar[s] for s in serves], topo))
+                         for k, serves in VIA[item[0]] if f in serves][0]
+                g.tensor.wait_ge(T.sem["%s_%d" % (item, j)], n)
+        b = WT * j + i
+        if (j, i) in halved:
+            e = spare[halved.index((j, i))]
+            g.tensor.matmul_mx(T.ps[:, BANK * b:BANK * b + HC], codes(j, i), plane(j, i), T.xc[:, 0:HC], T.xs[:, 0:HC],
+                               True, True).then_inc(T.sem["m_%d" % b], 1)
+            g.tensor.wait_ge(T.sem["e_%d" % e], 1)
+            g.tensor.matmul_mx(T.ps[:, BANK * e:BANK * e + HC], codes(j, i), plane(j, i), T.xc[:, HC:NC], T.xs[:, HC:NC],
+                               True, True).then_inc(T.sem["n_%d" % b], 1)
+        else:
+            g.tensor.matmul_mx(T.ps[:, BANK * b:BANK * b + NC], codes(j, i), plane(j, i), T.xc[:], T.xs[:],
+                               True, True).then_inc(T.sem["m_%d" % b], 1)
+
+    stores = []
+
+    def store(q, b, n, sems):
+        for s in sems:
+            q.wait_ge(T.sem[s], 1)
+        q.dma_start(T.y[:, NC * b:NC * (b + n)], T.yt[:, NC * b:NC * (b + n)]).then_inc(T.sem["s_%d" % b], 16)
+        stores.append((q, "s_%d" % b))
+
+    for k, (j, i) in enumerate(whole):
+        b = WT * j + i
+        yo, po = T.yt[:, NC * b:NC * b + NC], T.ps[:, BANK * b:BANK * b + NC]
+        if k % 2 == 0:
+            g.vector.wait_ge(T.sem["m_%d" % b], 1)
+            g.vector.tensor_copy(yo, po).then_inc(T.sem["e_%d" % b], 1)
+        else:
+            g.scalar.wait_ge(T.sem["m_%d" % b], 1)
+            g.scalar.activation(yo, po, ActivationFunctionType.Copy).then_inc(T.sem["e_%d" % b], 1)
+        if j != r:
+            store(g.sync, b, 1, ["e_%d" % b])
+        elif i == WT - 1:
+            store(g.sync, WT * r, WT, ["e_%d" % (WT * r + t) for t in range(WT)])
+    for k, (j, i) in enumerate(halved):
+        b, e = WT * j + i, spare[k]
+        g.vector.wait_ge(T.sem["m_%d" % b], 1)
+        g.vector.tensor_copy(T.yt[:, NC * b:NC * b + HC], T.ps[:, BANK * b:BANK * b + HC]).then_inc(T.sem["e_%d" % b], 1)
+        g.scalar.wait_ge(T.sem["n_%d" % b], 1)
+        g.scalar.activation(T.yt[:, NC * b + HC:NC * b + NC], T.ps[:, BANK * e:BANK * e + HC],
+                            ActivationFunctionType.Copy).then_inc(T.sem["f_%d" % b], 1)
+        store(g.scalar if k == len(halved) - 1 else g.sync, b, 1, ["e_%d" % b, "f_%d" % b])
+    for q, s in stores:
+        q.wait_ge(T.sem[s], 16)

from concourse.bass import DstId, RemoteDMATransfer
from concourse.mybir import dt, AluOpType, ActivationFunctionType

N, WT, NC, TW = 4, 2, 256, 512
SIM_CORES = 256
QW = TW // 4
HC = NC // 2
BANK = 512
CUT = 352
ITEMS = ("c0", "p0", "c1", "p1")
VIA = {"c": ((0, (0,)), (1, (1,))), "p": ((2, (0, 1)),)}

SCRATCH = {
    "wt": ("sbuf", [128, WT * TW], "bfloat16"),
    "gt": ("sbuf", [128, WT * TW], "bfloat16"),
    "gs": ("sbuf", [128, WT * TW], "bfloat16"),
    "vt": ("sbuf", [128, WT * TW], "bfloat16"),
    "xt": ("sbuf", [128, 4 * NC], "bfloat16"),
    "xc": ("sbuf", [128, NC], "float8_e4m3fn_x4"),
    "xs": ("sbuf", [128, NC], "uint8"),
    "yt": ("sbuf", [128, N * WT * NC], "float32"),
    "ps": ("psum", [128, BANK * N * WT], "float32"),
}
for _j in range(N):
    SCRATCH["cd%d" % _j] = ("sbuf", [128, WT * QW], "float8_e4m3fn_x4")
    SCRATCH["pl%d" % _j] = ("sbuf", [128, WT * QW], "uint8")

SEMAPHORES = ["lw0", "lw1", "lg0", "lg1", "lx", "gs0", "gs0b", "gs1", "v0", "v1", "q0", "q1", "qx", "sent"]
for _j in range(N):
    SEMAPHORES += ["%s_%d" % (_it, _j) for _it in ITEMS]
for _b in range(N * WT):
    SEMAPHORES += ["m_%d" % _b, "n_%d" % _b, "e_%d" % _b, "f_%d" % _b, "s_%d" % _b]


def _bits(mask):
    return bin(mask).count("1")


def _plan(src, cores, topo):
    peers = [c for c in cores if c != src]
    near = [c for c in peers if topo.may_write(src, c)]
    far = sorted((c for c in peers if not topo.may_write(src, c)), key=lambda c: topo.host(c) != topo.host(src))
    fit = [c for c in range(SIM_CORES)
           if topo.host(c) == topo.host(src) and topo.chip(c) == topo.chip(src) and c not in cores
           and all(topo.may_write(c, d) for d in far)]
    own = [c for c in fit if topo.die(c) == topo.die(src)]
    other = [c for c in fit if topo.die(c) != topo.die(src)]
    return near, far, [other[0], own[0], other[1]]


def _common(src, dsts, topo):
    mask = topo.mask(src, dsts[0])
    for d in dsts:
        mask &= topo.mask(src, d)
    return mask


def _relay_mask(src, item, cores, topo):
    near, _, relays = _plan(src, cores, topo)
    mask = _common(src, relays, topo)
    return mask & ~_common(src, near, topo) if item[1] == "0" else mask


def rank_program(g, core, T, topo):
    cores = [int(c) for c in T.cores]

    def codes(j, i):
        return T["cd%d" % j][:, i * QW:(i + 1) * QW]

    def plane(j, i):
        return T["pl%d" % j][:, i * QW:(i + 1) * QW]

    def send(j, item, dsts, mask):
        i = int(item[1])
        view = codes(j, i).bitcast(dt.uint8) if item[0] == "c" else plane(j, i)
        ids = []
        for d in dsts:
            rid, pid = topo.addr(d, core)
            ids.append(DstId(rid=rid, pnc=pid))
        g.remote_dma_fused([RemoteDMATransfer(dst_ids=ids, dma_engine_mask=mask, remote_sem=T.sem["%s_%d" % (item, j)],
                                              srcs=[view], dsts=[view for d in dsts])], local_sem=T.sem.sent)
        return _bits(mask)

    rank = T.rank_of(core)
    if rank is None:
        for j, src in enumerate(cores):
            _, far, relays = _plan(src, cores, topo)
            sent = 0
            for item in ITEMS:
                for k, serves in VIA[item[0]]:
                    if relays[k] == core:
                        dsts = [far[f] for f in serves]
                        g.wait_ge(T.sem["%s_%d" % (item, j)], _bits(_relay_mask(src, item, cores, topo)))
                        sent += send(j, item, dsts, _common(core, dsts, topo))
            if sent:
                g.wait_ge(T.sem.sent, sent)
        return

    near, far, relays = _plan(core, cores, topo)
    r = rank
    t0, t1 = slice(0, TW), slice(TW, 2 * TW)

    g.sync.dma_start(T.gt[:, t0], T.gr[:, t0]).then_inc(T.sem.lg0, 16)
    g.scalar.dma_start(T.wt[:, t0], T.w[:, t0]).then_inc(T.sem.lw0, 16)
    g.sync.dma_start(T.gt[:, t1], T.gr[:, t1]).then_inc(T.sem.lg1, 16)
    g.scalar.dma_start(T.wt[:, t1], T.w[:, t1]).then_inc(T.sem.lw1, 16)
    g.sync.dma_start(T.xt[:], T.x[:]).then_inc(T.sem.lx, 16)

    a, b = slice(0, CUT), slice(CUT, TW)
    g.scalar.wait_ge(T.sem.lg0, 16)
    g.scalar.activation(T.gs[:, b], T.gt[:, b], ActivationFunctionType.Copy, scale=0.25).then_inc(T.sem.gs0b, 1)
    g.scalar.wait_ge(T.sem.lg1, 16)
    g.scalar.activation(T.gs[:, t1], T.gt[:, t1], ActivationFunctionType.Copy, scale=0.25).then_inc(T.sem.gs1, 1)
    g.vector.wait_ge(T.sem.lg0, 16)
    g.vector.tensor_scalar(T.gs[:, a], T.gt[:, a], 0.25, None, AluOpType.mult).then_inc(T.sem.gs0, 1)
    for i, t in ((0, t0), (1, t1)):
        g.vector.wait_ge(T.sem["lw%d" % i], 16)
        g.vector.wait_ge(T.sem["gs%d" % i], 1)
        if i == 0:
            g.vector.wait_ge(T.sem.gs0b, 1)
        g.vector.tensor_tensor(T.vt[:, t], T.wt[:, t], T.gs[:, t], AluOpType.subtract).then_inc(T.sem["v%d" % i], 1)
        g.vector.wait_ge(T.sem["v%d" % i], 1)
        g.vector.quantize_mx(codes(r, i), plane(r, i), T.vt[:, t]).then_inc(T.sem["q%d" % i], 1)
    g.vector.wait_ge(T.sem.lx, 16)
    g.vector.quantize_mx(T.xc[:], T.xs[:], T.xt[:]).then_inc(T.sem.qx, 1)

    near_mask = _common(core, near, topo)
    sent = 0
    for i in range(WT):
        g.wait_ge(T.sem["q%d" % i], 1)
        items = ["c%d" % i, "p%d" % i]
        for item in items:
            sent += send(r, item, [relays[k] for k, _ in VIA[item[0]]], _relay_mask(core, item, cores, topo))
        for item in items:
            sent += send(r, item, near, near_mask)
    g.wait_ge(T.sem.sent, sent)

    nearj, farj = [cores.index(c) for c in near], [cores.index(c) for c in far]
    whole = [(j, i) for j in [r] + nearj for i in range(WT)] + [(j, 0) for j in farj]
    halved = [(j, 1) for j in farj]
    spare = [WT * r + k for k in range(len(halved))]

    g.tensor.wait_ge(T.sem.qx, 1)
    for j, i in whole + halved:
        src = cores[j]
        if j == r:
            g.tensor.wait_ge(T.sem["q%d" % i], 1)
        else:
            for item in ("c%d" % i, "p%d" % i):
                if j in nearj:
                    n = _bits(_common(src, [core], topo))
                else:
                    _, jfar, jrelays = _plan(src, cores, topo)
                    f = jfar.index(core)
                    n = [_bits(_common(jrelays[k], [jfar[s] for s in serves], topo))
                         for k, serves in VIA[item[0]] if f in serves][0]
                g.tensor.wait_ge(T.sem["%s_%d" % (item, j)], n)
        b = WT * j + i
        if (j, i) in halved:
            e = spare[halved.index((j, i))]
            g.tensor.matmul_mx(T.ps[:, BANK * b:BANK * b + HC], codes(j, i), plane(j, i), T.xc[:, 0:HC], T.xs[:, 0:HC],
                               True, True).then_inc(T.sem["m_%d" % b], 1)
            g.tensor.wait_ge(T.sem["e_%d" % e], 1)
            g.tensor.matmul_mx(T.ps[:, BANK * e:BANK * e + HC], codes(j, i), plane(j, i), T.xc[:, HC:NC], T.xs[:, HC:NC],
                               True, True).then_inc(T.sem["n_%d" % b], 1)
        else:
            g.tensor.matmul_mx(T.ps[:, BANK * b:BANK * b + NC], codes(j, i), plane(j, i), T.xc[:], T.xs[:],
                               True, True).then_inc(T.sem["m_%d" % b], 1)

    stores = []

    def store(q, b, n, sems):
        for s in sems:
            q.wait_ge(T.sem[s], 1)
        q.dma_start(T.y[:, NC * b:NC * (b + n)], T.yt[:, NC * b:NC * (b + n)]).then_inc(T.sem["s_%d" % b], 16)
        stores.append((q, "s_%d" % b))

    for k, (j, i) in enumerate(whole):
        b = WT * j + i
        yo, po = T.yt[:, NC * b:NC * b + NC], T.ps[:, BANK * b:BANK * b + NC]
        if k % 2 == 0:
            g.vector.wait_ge(T.sem["m_%d" % b], 1)
            g.vector.tensor_copy(yo, po).then_inc(T.sem["e_%d" % b], 1)
        else:
            g.scalar.wait_ge(T.sem["m_%d" % b], 1)
            g.scalar.activation(yo, po, ActivationFunctionType.Copy).then_inc(T.sem["e_%d" % b], 1)
        if j != r:
            store(g.sync, b, 1, ["e_%d" % b])
        elif i == WT - 1:
            store(g.sync, WT * r, WT, ["e_%d" % (WT * r + t) for t in range(WT)])
    for k, (j, i) in enumerate(halved):
        b, e = WT * j + i, spare[k]
        g.vector.wait_ge(T.sem["m_%d" % b], 1)
        g.vector.tensor_copy(T.yt[:, NC * b:NC * b + HC], T.ps[:, BANK * b:BANK * b + HC]).then_inc(T.sem["e_%d" % b], 1)
        g.scalar.wait_ge(T.sem["n_%d" % b], 1)
        g.scalar.activation(T.yt[:, NC * b + HC:NC * b + NC], T.ps[:, BANK * e:BANK * e + HC],
                            ActivationFunctionType.Copy).then_inc(T.sem["f_%d" % b], 1)
        store(g.scalar if k == len(halved) - 1 else g.sync, b, 1, ["e_%d" % b, "f_%d" % b])
    for q, s in stores:
        q.wait_ge(T.sem[s], 16)
